import numpy as np, ml_dtypes
CORES = [51,54,179,182]
N = 4
import mx_ref
BF = ml_dtypes.bfloat16
def entries(a):
    return np.ascontiguousarray(a.T).reshape(-1)
def table(e):
    return np.ascontiguousarray(np.reshape(e, (-1, 16)).T).astype(np.int32)
def cut(t, i, w=512):
    return t[:, w * i:w * i + w]
def f(rng, *shape):
    return mx_ref.flush((rng.standard_normal(shape, dtype=np.float32) * np.exp2(rng.integers(-2, 3, shape[:-1] + (1,)))).astype(BF))
def wide(rng, *shape, cols=0):
    v = rng.standard_normal(shape, dtype=np.float32) * np.exp2(rng.integers(-12, 13, shape)).astype(np.float32)
    if cols: v *= np.repeat(np.exp2(rng.integers(-cols, cols + 1, shape[:-2] + (1, shape[-1] // 4))) * (rng.random(shape[:-2] + (1, shape[-1] // 4)) > 0.0625), 4, axis=-1).astype(np.float32)
    return mx_ref.flush(v.astype(BF))
E, NB = 3, 4
T, L, G = 128 * NB, 4 * NB, N * E
def listed(es):
    return {"ids": np.stack([table(e) for e in es])}
def setup_inputs(rng):
    return {"x": f(rng, N, 128, 4 * T), "wt": f(rng, N, 128, 512 * E), **listed([rng.integers(0, G, L) for r in range(N)])}
def setup_inputs_one(rng):
    return {**setup_inputs(rng), **listed([np.full(L, rng.integers(0, G))] * N)}
def setup_inputs_own(rng):
    return {**setup_inputs(rng), **listed([r * E + rng.integers(0, E, L) for r in range(N)])}
def setup_inputs_ends(rng):
    es = []
    for r in range(N):
        e = rng.choice([0, G - 1], L); e[rng.permutation(L)[:2]] = [0, G - 1]
        es.append(e)
    return {**setup_inputs(rng), **listed(es)}
def setup_inputs_each(rng):
    return {**setup_inputs(rng), **listed([np.concatenate([rng.permutation(G) for i in range(L // G + 1)])[:L] for r in range(N)])}
def setup_inputs_spread(rng):
    d = setup_inputs(rng); d["x"] = wide(rng, N, 128, 4 * T, cols=8); d["wt"] = wide(rng, N, 128, 512 * E, cols=8); return d
def check_inputs(d):
    b = []
    for r in range(N):
        e = entries(d["ids"][r])
        if e.min() < 0 or e.max() >= G: b.append("ids")
    return b
def reference(x, wt, ids):
    U = [mx_ref.quantize(np.ascontiguousarray(cut(wt[q], m))) for q in range(N) for m in range(E)]
    y = np.zeros((N, 128, 4 * T), np.float32)
    for r in range(N):
        e = entries(ids[r])
        for b in range(NB):
            X = mx_ref.quantize(np.ascontiguousarray(cut(x[r], b)))
            for k in range(4):
                c = 128 * (k * NB + b)
                y[r][:, c:c + 128] = mx_ref.matmul(U[e[4 * b + k]], X)
    return {"y": y}

@@ -1,0 +1,187 @@
+import numpy as np
+from concourse.bass import DstId, RemoteDMATransfer
+from concourse.mybir import dt, AluOpType, ActivationFunctionType
+
+N, E, NB = 4, 3, 4
+H = 2
+C = 128 // H
+PW = E * C
+WIN = N * PW
+SW = 4 * C
+n16 = C // 16
+
+SCRATCH = {
+    "idrow": ("sbuf", [1, 16], "int32"),
+    "idb": ("sbuf", [128, 16], "int32"),
+    "io1": ("sbuf", [128, C // 16], "int32"),
+    "io2": ("sbuf", [128, C // 16], "int32"),
+    "io3": ("sbuf", [128, C // 16], "int32"),
+    "colf": ("sbuf", [128, C // 16], "float32"),
+    "off": ("sbuf", [128, C], "uint16"),
+    "wb0": ("sbuf", [128, 4 * PW], "bfloat16"),
+    "wb1": ("sbuf", [128, 4 * PW], "bfloat16"),
+    "xb": ("sbuf", [128, 2048], "bfloat16"),
+    "xq": ("sbuf", [128, 512], "float8_e4m3fn_x4"),
+    "xs": ("sbuf", [128, 512], "uint8"),
+    "wc0": ("sbuf", [128, WIN], "float8_e4m3fn_x4"),
+    "wc1": ("sbuf", [128, WIN], "float8_e4m3fn_x4"),
+    "ws0": ("sbuf", [128, WIN], "uint8"),
+    "ws1": ("sbuf", [128, WIN], "uint8"),
+    "slotc": ("sbuf", [128, 2048], "float8_e4m3fn_x4"),
+    "slots": ("sbuf", [128, 2048], "uint8"),
+    "yo": ("sbuf", [128, 2048], "float32"),
+    "ps": ("psum", [128, 4096], "float32"),
+}
+SEMAPHORES = (["ldi", "ldw0", "ldw1", "ldx", "iota", "bc", "a1", "a2", "offs", "q0", "q1", "qx",
+               "c0", "c1", "s0", "s1", "loc", "sty", "sta"]
+              + ["pc%d%d" % (h, b) for h in range(H) for b in range(NB)]
+              + ["pk%d%d" % (h, b) for h in range(H) for b in range(NB)]
+              + ["mm%d%d%d" % (h, b, k) for h in range(H) for b in range(NB) for k in range(2)]
+              + ["ev%d%d%d" % (h, b, k) for h in range(H) for b in range(NB) for k in range(2)])
+
+
+def bits(engines):
+    m = 0
+    for e in engines:
+        m |= 1 << e
+    return m
+
+
+def rank_program(g, core, T, topo):
+    r = T.rank_of(core)
+    if r is None:
+        return
+    S = T.sem
+    V, A, Y, P = g.vector, g.scalar, g.sync, g.tensor
+    ADD, MUL = AluOpType.add, AluOpType.mult
+    COPY = ActivationFunctionType.Copy
+    here = topo.cores_of(core)
+    mate_core = [c for c in T.cores if c != core and c in here][0]
+    far = [c for c in T.cores if c not in here]
+
+    def load_w(q, h, m):
+        q.dma_start(T["wb%d" % h][:, 4 * C * m:4 * C * (m + 1)],
+                    T.wt[:, 512 * m + 4 * C * h:512 * m + 4 * C * (h + 1)]).then_inc(S["ldw%d" % h], 16)
+    load_w(Y, 0, 0)
+    load_w(A, 0, 1)
+    load_w(Y, 0, 2)
+    A.dma_start(T.idrow[:], T.ids[:]).then_inc(S.ldi, 16)
+    load_w(Y, 1, 0)
+    load_w(A, 1, 1)
+    load_w(Y, 1, 2)
+    A.dma_start(T.xb[:, 0:1024], T.x[:, 0:1024]).then_inc(S.ldx, 16)
+    Y.dma_start(T.xb[:, 1024:2048], T.x[:, 1024:2048]).then_inc(S.ldx, 16)
+
+    g.iota(T.io1[:], [[0, C // 16]], 0, 1).then_inc(S.iota, 1)
+    g.iota(T.io2[:], [[16, C // 16]], 0, 0).then_inc(S.iota, 1)
+    g.wait_ge(S.ldi, 16)
+    g.partition_broadcast(T.idb[:], T.idrow[:], 128).then_inc(S.bc, 1)
+
+    off_e = topo.engines(core, far[0])
+    on_e = [e for e in topo.engines(core, mate_core) if e not in off_e]
+    half = len(off_e) // 2
+    ways = [(far[0], off_e[:half]), (far[1], off_e[half:]), (mate_core, on_e)]
+
+    def send(ap, sem):
+        ts = []
+        for dst, eng in ways:
+            rid, pid = topo.addr(dst, core)
+            ts.append(RemoteDMATransfer(dst_ids=[DstId(rid=rid, pnc=pid)], dma_engine_mask=bits(eng), remote_sem=sem,
+                                        src=ap, dst=ap))
+        g.remote_dma_fused(ts, local_sem=S.loc)
+    arrived = 2 * half + len(on_e)
+    own = slice(PW * r, PW * (r + 1))
+    for h in range(H):
+        g.wait_ge(S["q%d" % h], 1)
+        send(T["wc%d" % h][:, own].bitcast(dt.uint8), S["c%d" % h])
+        send(T["ws%d" % h][:, own], S["s%d" % h])
+
+    V.wait_ge(S.iota, 2)
+    V.tensor_scalar(T.io3[:], T.io1[:], 15, None, AluOpType.bitwise_and).then_inc(S.a1, 1)
+    V.wait_ge(S.a1, 1)
+    V.tensor_tensor(T.colf[:], T.io3[:], T.io2[:], ADD).then_inc(S.a2, 1)
+    for h in range(H):
+        V.wait_ge(S["ldw%d" % h], 48)
+        V.quantize_mx(T["wc%d" % h][:, own], T["ws%d" % h][:, own], T["wb%d" % h][:]).then_inc(S["q%d" % h], 1)
+    V.wait_ge(S.bc, 1)
+    V.wait_ge(S.a2, 1)
+    for i in range(n16):
+        V.tensor_scalar(T.off[:, i:C:n16], T.idb[:], float(C), T.colf[:, i:i + 1], MUL, ADD).then_inc(S.offs, 1)
+    V.wait_ge(S.ldx, 32)
+    V.quantize_mx(T.xq[:], T.xs[:], T.xb[:]).then_inc(S.qx, 1)
+
+    def slot(h, b):
+        return 1024 * h + SW * b
+
+    def pick_c(h, b):
+        if b == 0:
+            if h == 0:
+                V.wait_ge(S.offs, n16)
+            V.wait_ge(S["q%d" % h], 1)
+            V.wait_ge(S["c%d" % h], arrived)
+        a = slot(h, b)
+        V.tensor_copy(T.slotc[:, a:a + SW].bitcast(dt.uint32),
+                      T["wc%d" % h][:, 0:WIN].bitcast(dt.uint32).indirect(T.off[:, SW // 16 * b:SW // 16 * (b + 1)])
+                      ).then_inc(S["pc%d%d" % (h, b)], 1)
+
+    def pick_s(h, b):
+        if b == 0:
+            if h == 0:
+                A.wait_ge(S.offs, n16)
+            A.wait_ge(S["q%d" % h], 1)
+            A.wait_ge(S["s%d" % h], arrived)
+        a = slot(h, b)
+        A.activation(T.slots[:, a:a + SW],
+                     T["ws%d" % h][:, 0:WIN].indirect(T.off[:, SW // 16 * b:SW // 16 * (b + 1)]),
+                     COPY).then_inc(S["pk%d%d" % (h, b)], 1)
+
+    def product(h, b):
+        if b == 0 and h == 0:
+            P.wait_ge(S.qx, 1)
+        P.wait_ge(S["pc%d%d" % (h, b)], 1)
+        P.wait_ge(S["pk%d%d" % (h, b)], 1)
+        for k in range(2):
+            if h:
+                P.wait_ge(S["ev%d%d%d" % (h - 1, b, k)], 1)
+            a, o = slot(h, b) + 128 * k, 512 * (2 * b + k)
+            P.matmul_mx(T.ps[:, o:o + 128], T.slotc[:, a:a + 128], T.slots[:, a:a + 128],
+                        T.xq[:, 128 * b:128 * (b + 1)], T.xs[:, 128 * b:128 * (b + 1)], True, True
+                        ).then_inc(S["mm%d%d%d" % (h, b, k)], 1)
+
+    def evac(h, b, k):
+        o, w = 512 * (2 * b + k), 512 * (2 * h + k) + 128 * b
+        q = A if k else V
+        q.wait_ge(S["mm%d%d%d" % (h, b, k)], 1)
+        if k:
+            c = A.activation(T.yo[:, w:w + 128], T.ps[:, o:o + 128], COPY)
+        else:
+            c = V.tensor_copy(T.yo[:, w:w + 128], T.ps[:, o:o + 128])
+        c.then_inc(S["ev%d%d%d" % (h, b, k)], 1)
+
+    for h in range(H):
+        for b in range(NB):
+            pick_c(h, b)
+            pick_s(h, b)
+            product(h, b)
+            if b:
+                evac(h, b - 1, 0)
+                evac(h, b - 1, 1)
+        evac(h, NB - 1, 0)
+        evac(h, NB - 1, 1)
+
+    def store(q, sem, h, k, b0, b1):
+        for b in range(b0, b1):
+            q.wait_ge(S["ev%d%d%d" % (h, b, k)], 1)
+        for u in range(2):
+            w, c = 512 * (2 * h + k), 512 * (2 * k + u)
+            q.dma_start(T.y[64 * h:64 * (h + 1), c + 128 * b0:c + 128 * b1],
+                        T.yo[64 * u:64 * (u + 1), w + 128 * b0:w + 128 * b1]).then_inc(S[sem], 16)
+    store(Y, "sty", 0, 0, 0, 4)
+    store(Y, "sty", 0, 1, 0, 4)
+    store(Y, "sty", 1, 0, 0, 2)
+    store(Y, "sty", 1, 1, 0, 2)
+    store(Y, "sty", 1, 0, 2, 4)
+    store(A, "sta", 1, 1, 2, 4)
+    Y.wait_ge(S.sty, 16 * 10)
+    A.wait_ge(S.sta, 16 * 2)
+    g.wait_ge(S.loc, 2 * H * arrived)

@@ -3,41 +3,56 @@ from concourse.bass import DstId, RemoteDMATransfer
 from concourse.mybir import dt, AluOpType, ActivationFunctionType
 
 N, E, NB = 4, 3, 4
-H = 2
-C = 128 // H
-PW = E * C
-WIN = N * PW
-SW = 4 * C
-n16 = C // 16
+Q = 32
+NQ = 128 // Q
+PIECES = [(0, 2), (2, 1), (3, 1)]
+HANDED = ["c2", "s2"]
+SPANS = {0: [(0, 4)], 1: [(0, 4)], 2: [(0, 4)], 3: [(0, 2), (2, 3), (3, 4)]}
+ON_VECTOR = "s10 c00 c10 c20 c30 c31 c32 e23 e31 e33".split()
+ON_SCALAR = "s00 s20 e00 e01 e02 e03 s30 s31 s32 e10 e11 e12 e13 e20 e21 e22 e30 e32".split()
+WIDTHS = sorted(set(w for q0, w in PIECES))
+
+
+def slot(w):
+    return max(E * Q * w, 128)
+
 
 SCRATCH = {
     "idrow": ("sbuf", [1, 16], "int32"),
     "idb": ("sbuf", [128, 16], "int32"),
-    "io1": ("sbuf", [128, C // 16], "int32"),
-    "io2": ("sbuf", [128, C // 16], "int32"),
-    "io3": ("sbuf", [128, C // 16], "int32"),
-    "colf": ("sbuf", [128, C // 16], "float32"),
-    "off": ("sbuf", [128, C], "uint16"),
-    "wb0": ("sbuf", [128, 4 * PW], "bfloat16"),
-    "wb1": ("sbuf", [128, 4 * PW], "bfloat16"),
+    "io1": ("sbuf", [128, 16], "int32"),
+    "io2": ("sbuf", [128, 8], "int32"),
+    "io3": ("sbuf", [128, 8], "int32"),
+    "low": ("sbuf", [128, 16], "int32"),
+    "mask": ("sbuf", [128, 16], "float32"),
+    "sub": ("sbuf", [128, 8], "int32"),
+    "colf": ("sbuf", [128, 8], "float32"),
+    "t16": ("sbuf", [128, 16], "float32"),
+    "t8": ("sbuf", [128, 8], "float32"),
+    "sel": ("sbuf", [128, 4], "float32"),
+    "third": ("sbuf", [128, 4], "float32"),
+    "rk": ("sbuf", [128, 4], "int32"),
     "xb": ("sbuf", [128, 2048], "bfloat16"),
     "xq": ("sbuf", [128, 512], "float8_e4m3fn_x4"),
     "xs": ("sbuf", [128, 512], "uint8"),
-    "wc0": ("sbuf", [128, WIN], "float8_e4m3fn_x4"),
-    "wc1": ("sbuf", [128, WIN], "float8_e4m3fn_x4"),
-    "ws0": ("sbuf", [128, WIN], "uint8"),
-    "ws1": ("sbuf", [128, WIN], "uint8"),
     "slotc": ("sbuf", [128, 2048], "float8_e4m3fn_x4"),
     "slots": ("sbuf", [128, 2048], "uint8"),
     "yo": ("sbuf", [128, 2048], "float32"),
     "ps": ("psum", [128, 4096], "float32"),
 }
-SEMAPHORES = (["ldi", "ldw0", "ldw1", "ldx", "iota", "bc", "a1", "a2", "offs", "q0", "q1", "qx",
-               "c0", "c1", "s0", "s1", "loc", "sty", "sta"]
-              + ["pc%d%d" % (h, b) for h in range(H) for b in range(NB)]
-              + ["pk%d%d" % (h, b) for h in range(H) for b in range(NB)]
-              + ["mm%d%d%d" % (h, b, k) for h in range(H) for b in range(NB) for k in range(2)]
-              + ["ev%d%d%d" % (h, b, k) for h in range(H) for b in range(NB) for k in range(2)])
+for w in WIDTHS:
+    SCRATCH["tl%d" % w] = ("sbuf", [128, 4], "float32")
+    SCRATCH["sl%d" % w] = ("sbuf", [128, 4], "float32")
+    SCRATCH["off%d" % w] = ("sbuf", [128, 8 * NB], "uint16")
+for pi, (q0, w) in enumerate(PIECES):
+    SCRATCH["wb%d" % pi] = ("sbuf", [128, 4 * slot(w)], "bfloat16")
+    SCRATCH["ws%d" % pi] = ("sbuf", [128, N * slot(w)], "uint8")
+    SCRATCH["wc%d" % pi] = ("sbuf", [128, N * slot(w)], "float8_e4m3fn_x4")
+
+SEMAPHORES = (["ldi", "ldx", "iota", "bc", "zero", "step", "offs", "offs2", "qx", "loc", "sty"]
+              + ["%s%d" % (s, i) for s in ("ldw", "q", "c", "s") for i in range(len(PIECES))]
+              + ["%s%d%d" % (s, q, i) for s in ("pc", "ps") for q in range(NQ) for i in range(len(SPANS[q]))]
+              + ["%s%d%d" % (s, q, b) for s in ("mm", "ev") for q in range(NQ) for b in range(NB)])
 
 
 def bits(engines):
@@ -47,141 +62,194 @@ def bits(engines):
     return m
 
 
+def helpers(core, T, topo):
+    free = [c for c in topo.cores_of(core) if c not in T.cores and topo.die(c) == topo.die(core)]
+    return free[:len(HANDED)]
+
+
+def to_far(src, item, T, topo):
+    far = [c for c in T.cores if c not in topo.cores_of(src)]
+    eng = topo.engines(src, far[0])
+    half = len(eng) // 2
+    return [(item, far[0], eng[:half]), (item, far[1], eng[half:])]
+
+
+def hand_on(core, h, T, topo):
+    return to_far(helpers(core, T, topo)[h], HANDED[h], T, topo)
+
+
+def calls_of(core, T, topo):
+    near = [c for c in T.cores if c != core and c in topo.cores_of(core)][0]
+    off = [e for item, dst, eng in to_far(core, "c0", T, topo) for e in eng]
+    on = [e for e in topo.engines(core, near) if e not in off]
+    a, b = on[0::2], on[1::2]
+    hc, hs = helpers(core, T, topo)
+    return [to_far(core, "s0", T, topo) + [("s0", near, a)],
+            to_far(core, "c0", T, topo) + [("c0", near, a)],
+            to_far(core, "s1", T, topo) + [("s1", near, a), ("s2", hs, b[:2]), ("s2", near, b[2:])],
+            to_far(core, "c1", T, topo) + [("c1", near, a), ("c2", hc, b)],
+            [("c2", near, b)]]
+
+
+def send(g, core, r, call, T, topo):
+    ts = []
+    for item, dst, eng in call:
+        w = PIECES[int(item[1])][1]
+        ap = T["w" + item][:, slot(w) * r:slot(w) * r + E * Q * w]
+        ap = ap.bitcast(dt.uint8) if item[0] == "c" else ap
+        rid, pid = topo.addr(dst, core)
+        ts.append(RemoteDMATransfer(dst_ids=[DstId(rid=rid, pnc=pid)], dma_engine_mask=bits(eng),
+                                    remote_sem=T.sem[item], src=ap, dst=ap))
+    g.remote_dma_fused(ts, local_sem=T.sem.loc)
+
+
+def helper_program(g, core, T, topo):
+    for r, rank in enumerate(T.cores):
+        if core in helpers(rank, T, topo):
+            call = hand_on(rank, helpers(rank, T, topo).index(core), T, topo)
+            got = sum(len(eng) for c in calls_of(rank, T, topo) for item, dst, eng in c if dst == core)
+            g.wait_ge(T.sem[call[0][0]], got)
+            send(g, core, r, call, T, topo)
+            g.wait_ge(T.sem.loc, sum(len(eng) for item, dst, eng in call))
+
+
 def rank_program(g, core, T, topo):
     r = T.rank_of(core)
     if r is None:
-        return
+        return helper_program(g, core, T, topo)
     S = T.sem
     V, A, Y, P = g.vector, g.scalar, g.sync, g.tensor
     ADD, MUL = AluOpType.add, AluOpType.mult
     COPY = ActivationFunctionType.Copy
-    here = topo.cores_of(core)
-    mate_core = [c for c in T.cores if c != core and c in here][0]
-    far = [c for c in T.cores if c not in here]
 
-    def load_w(q, h, m):
-        q.dma_start(T["wb%d" % h][:, 4 * C * m:4 * C * (m + 1)],
-                    T.wt[:, 512 * m + 4 * C * h:512 * m + 4 * C * (h + 1)]).then_inc(S["ldw%d" % h], 16)
-    load_w(Y, 0, 0)
-    load_w(A, 0, 1)
-    load_w(Y, 0, 2)
     A.dma_start(T.idrow[:], T.ids[:]).then_inc(S.ldi, 16)
-    load_w(Y, 1, 0)
-    load_w(A, 1, 1)
-    load_w(Y, 1, 2)
-    A.dma_start(T.xb[:, 0:1024], T.x[:, 0:1024]).then_inc(S.ldx, 16)
-    Y.dma_start(T.xb[:, 1024:2048], T.x[:, 1024:2048]).then_inc(S.ldx, 16)
+    queues = [Y, Y, A, A, Y, A]
+    n = 0
+    for pi, (q0, w) in enumerate(PIECES):
+        for m in range(E):
+            a, c = 4 * Q * w * m, 512 * m + 4 * Q * q0
+            queues[n % len(queues)].dma_start(T["wb%d" % pi][:, a:a + 4 * Q * w], T.wt[:, c:c + 4 * Q * w]
+                                              ).then_inc(S["ldw%d" % pi], 16)
+            n += 1
+    Y.dma_start(T.xb[:], T.x[:]).then_inc(S.ldx, 16)
 
-    g.iota(T.io1[:], [[0, C // 16]], 0, 1).then_inc(S.iota, 1)
-    g.iota(T.io2[:], [[16, C // 16]], 0, 0).then_inc(S.iota, 1)
+    g.iota(T.io1[:], [[0, 4], [1, 4]], 128, -1).then_inc(S.iota, 1)
+    g.iota(T.io2[:], [[0, 8]], 0, 1).then_inc(S.iota, 1)
+    g.iota(T.io3[:], [[4, 8]], 0, 0).then_inc(S.iota, 1)
     g.wait_ge(S.ldi, 16)
     g.partition_broadcast(T.idb[:], T.idrow[:], 128).then_inc(S.bc, 1)
 
-    off_e = topo.engines(core, far[0])
-    on_e = [e for e in topo.engines(core, mate_core) if e not in off_e]
-    half = len(off_e) // 2
-    ways = [(far[0], off_e[:half]), (far[1], off_e[half:]), (mate_core, on_e)]
+    plan = calls_of(core, T, topo)
+    seen = set()
+    for call in plan:
+        for item, dst, eng in call:
+            if item[1] not in seen:
+                g.wait_ge(S["q" + item[1]], 1)
+                seen.add(item[1])
+        send(g, core, r, call, T, topo)
+    arrived = {}
+    for other in T.cores:
+        for call in calls_of(other, T, topo) + [hand_on(other, h, T, topo) for h in range(len(HANDED))]:
+            for item, dst, eng in call:
+                if dst == core:
+                    arrived[item] = arrived.get(item, 0) + len(eng)
 
-    def send(ap, sem):
-        ts = []
-        for dst, eng in ways:
-            rid, pid = topo.addr(dst, core)
-            ts.append(RemoteDMATransfer(dst_ids=[DstId(rid=rid, pnc=pid)], dma_engine_mask=bits(eng), remote_sem=sem,
-                                        src=ap, dst=ap))
-        g.remote_dma_fused(ts, local_sem=S.loc)
-    arrived = 2 * half + len(on_e)
-    own = slice(PW * r, PW * (r + 1))
-    for h in range(H):
-        g.wait_ge(S["q%d" % h], 1)
-        send(T["wc%d" % h][:, own].bitcast(dt.uint8), S["c%d" % h])
-        send(T["ws%d" % h][:, own], S["s%d" % h])
+    narrow = [pi for pi, (q0, w) in enumerate(PIECES) if slot(w) > E * Q * w]
+    for pi in narrow:
+        V.memset(T["wb%d" % pi][:, 4 * E * Q * PIECES[pi][1]:], 0.0).then_inc(S.zero, 1)
+    steps = [0]
 
-    V.wait_ge(S.iota, 2)
-    V.tensor_scalar(T.io3[:], T.io1[:], 15, None, AluOpType.bitwise_and).then_inc(S.a1, 1)
-    V.wait_ge(S.a1, 1)
-    V.tensor_tensor(T.colf[:], T.io3[:], T.io2[:], ADD).then_inc(S.a2, 1)
-    for h in range(H):
-        V.wait_ge(S["ldw%d" % h], 48)
-        V.quantize_mx(T["wc%d" % h][:, own], T["ws%d" % h][:, own], T["wb%d" % h][:]).then_inc(S["q%d" % h], 1)
+    def step(*calls):
+        for c in calls:
+            c.then_inc(S.step, 1)
+        steps[0] += len(calls)
+        V.wait_ge(S.step, steps[0])
+    V.wait_ge(S.iota, 3)
+    step(V.tensor_scalar(T.low[:], T.io1[:], 3, None, AluOpType.bitwise_and),
+         V.tensor_scalar(T.sub[:], T.io2[:], 15, 2, AluOpType.bitwise_and, AluOpType.logical_shift_right))
+    step(V.tensor_scalar(T.mask[:], T.low[:], 0.0, None, AluOpType.is_equal),
+         V.tensor_tensor(T.colf[:], T.sub[:], T.io3[:], ADD))
+    V.wait_ge(S.zero, len(narrow))
+    for pi, (q0, w) in enumerate(PIECES):
+        own = slice(slot(w) * r, slot(w) * (r + 1))
+        V.wait_ge(S["ldw%d" % pi], 16 * E)
+        V.quantize_mx(T["wc%d" % pi][:, own], T["ws%d" % pi][:, own], T["wb%d" % pi][:]).then_inc(S["q%d" % pi], 1)
     V.wait_ge(S.bc, 1)
-    V.wait_ge(S.a2, 1)
-    for i in range(n16):
-        V.tensor_scalar(T.off[:, i:C:n16], T.idb[:], float(C), T.colf[:, i:i + 1], MUL, ADD).then_inc(S.offs, 1)
-    V.wait_ge(S.ldx, 32)
+    step(V.tensor_tensor(T.t16[:], T.idb[:], T.mask[:], MUL))
+    step(V.tensor_tensor(T.t8[:], T.t16[:, 0:16:2], T.t16[:, 1:16:2], ADD))
+    step(V.tensor_tensor(T.sel[:], T.t8[:, 0:8:2], T.t8[:, 1:8:2], ADD))
+    step(V.tensor_scalar(T.third[:], T.sel[:], -1.0, 1.0 / E, ADD, MUL),
+         *[V.tensor_scalar(T["tl%d" % w][:], T.sel[:], float(Q * w), None, MUL) for w in WIDTHS])
+
+    def offsets(w, sem):
+        for b in range(NB):
+            more = [T["sl%d" % w][:, b:b + 1], ADD, ADD] if slot(w) > E * Q * w else [None, ADD]
+            V.tensor_scalar(T["off%d" % w][:, 8 * b:8 * b + 8], T.colf[:], T["tl%d" % w][:, b:b + 1], *more
+                            ).then_inc(sem, 1)
+    offsets(2, S.offs)
+    step(V.tensor_copy(T.rk[:], T.third[:]))
+    step(V.tensor_scalar(T.sl1[:], T.rk[:], float(slot(1) - E * Q), None, MUL))
+    offsets(1, S.offs2)
+    V.wait_ge(S.ldx, 16)
     V.quantize_mx(T.xq[:], T.xs[:], T.xb[:]).then_inc(S.qx, 1)
 
-    def slot(h, b):
-        return 1024 * h + SW * b
+    def piece_of(q):
+        return [pi for pi, (q0, w) in enumerate(PIECES) if q0 <= q < q0 + w][0]
 
-    def pick_c(h, b):
-        if b == 0:
-            if h == 0:
-                V.wait_ge(S.offs, n16)
-            V.wait_ge(S["q%d" % h], 1)
-            V.wait_ge(S["c%d" % h], arrived)
-        a = slot(h, b)
-        V.tensor_copy(T.slotc[:, a:a + SW].bitcast(dt.uint32),
-                      T["wc%d" % h][:, 0:WIN].bitcast(dt.uint32).indirect(T.off[:, SW // 16 * b:SW // 16 * (b + 1)])
-                      ).then_inc(S["pc%d%d" % (h, b)], 1)
+    def run(eng, order):
+        waited = set()
 
-    def pick_s(h, b):
-        if b == 0:
-            if h == 0:
-                A.wait_ge(S.offs, n16)
-            A.wait_ge(S["q%d" % h], 1)
-            A.wait_ge(S["s%d" % h], arrived)
-        a = slot(h, b)
-        A.activation(T.slots[:, a:a + SW],
-                     T["ws%d" % h][:, 0:WIN].indirect(T.off[:, SW // 16 * b:SW // 16 * (b + 1)]),
-                     COPY).then_inc(S["pk%d%d" % (h, b)], 1)
+        def wait(sem, count):
+            if sem not in waited:
+                eng.wait_ge(S[sem], count)
+                waited.add(sem)
+        for kind, q, i in [(o[0], int(o[1]), int(o[2])) for o in order]:
+            if kind == "e":
+                o, c = 512 * (NB * (q % 2) + i), 512 * q + 128 * i
+                wait("mm%d%d" % (q, i), 1)
+                if eng is V:
+                    call = V.tensor_copy(T.yo[:, c:c + 128], T.ps[:, o:o + 128])
+                else:
+                    call = A.activation(T.yo[:, c:c + 128], T.ps[:, o:o + 128], COPY)
+                call.then_inc(S["ev%d%d" % (q, i)], 1)
+                continue
+            pi = piece_of(q)
+            q0, w = PIECES[pi]
+            b0, b1 = SPANS[q][i]
+            lo, hi = Q * (q - q0), slot(w) * (N - 1) + E * Q * w
+            offs = T["off%d" % w][:, 8 * b0:8 * b1]
+            a, b = 512 * q + 128 * b0, 512 * q + 128 * b1
+            item = "%s%d" % (kind, pi)
+            wait("offs" if w == 2 else "offs2", NB)
+            wait("q%d" % pi, 1)
+            wait(item, arrived[item])
+            if kind == "c":
+                call = V.tensor_copy(T.slotc[:, a:b].bitcast(dt.uint32),
+                                     T["w" + item][:, lo:hi].bitcast(dt.uint32).indirect(offs))
+            elif eng is V:
+                call = V.tensor_copy(T.slots[:, a:b], T["w" + item][:, lo:hi].indirect(offs))
+            else:
+                call = A.activation(T.slots[:, a:b], T["w" + item][:, lo:hi].indirect(offs), COPY)
+            call.then_inc(S["p%s%d%d" % (kind, q, i)], 1)
+    run(V, ON_VECTOR)
+    run(A, ON_SCALAR)
 
-    def product(h, b):
-        if b == 0 and h == 0:
-            P.wait_ge(S.qx, 1)
-        P.wait_ge(S["pc%d%d" % (h, b)], 1)
-        P.wait_ge(S["pk%d%d" % (h, b)], 1)
-        for k in range(2):
-            if h:
-                P.wait_ge(S["ev%d%d%d" % (h - 1, b, k)], 1)
-            a, o = slot(h, b) + 128 * k, 512 * (2 * b + k)
-            P.matmul_mx(T.ps[:, o:o + 128], T.slotc[:, a:a + 128], T.slots[:, a:a + 128],
-                        T.xq[:, 128 * b:128 * (b + 1)], T.xs[:, 128 * b:128 * (b + 1)], True, True
-                        ).then_inc(S["mm%d%d%d" % (h, b, k)], 1)
+    P.wait_ge(S.qx, 1)
+    for q in range(NQ):
+        for i, (b0, b1) in enumerate(SPANS[q]):
+            P.wait_ge(S["pc%d%d" % (q, i)], 1)
+            P.wait_ge(S["ps%d%d" % (q, i)], 1)
+            for b in range(b0, b1):
+                if q >= 2:
+                    P.wait_ge(S["ev%d%d" % (q - 2, b)], 1)
+                a, o = 512 * q + 128 * b, 512 * (NB * (q % 2) + b)
+                P.matmul_mx(T.ps[:, o:o + 128], T.slotc[:, a:a + 128], T.slots[:, a:a + 128],
+                            T.xq[:, 128 * b:128 * (b + 1)], T.xs[:, 128 * b:128 * (b + 1)], True, True
+                            ).then_inc(S["mm%d%d" % (q, b)], 1)
 
-    def evac(h, b, k):
-        o, w = 512 * (2 * b + k), 512 * (2 * h + k) + 128 * b
-        q = A if k else V
-        q.wait_ge(S["mm%d%d%d" % (h, b, k)], 1)
-        if k:
-            c = A.activation(T.yo[:, w:w + 128], T.ps[:, o:o + 128], COPY)
-        else:
-            c = V.tensor_copy(T.yo[:, w:w + 128], T.ps[:, o:o + 128])
-        c.then_inc(S["ev%d%d%d" % (h, b, k)], 1)
-
-    for h in range(H):
+    for q in range(NQ):
         for b in range(NB):
-            pick_c(h, b)
-            pick_s(h, b)
-            product(h, b)
-            if b:
-                evac(h, b - 1, 0)
-                evac(h, b - 1, 1)
-        evac(h, NB - 1, 0)
-        evac(h, NB - 1, 1)
-
-    def store(q, sem, h, k, b0, b1):
-        for b in range(b0, b1):
-            q.wait_ge(S["ev%d%d%d" % (h, b, k)], 1)
-        for u in range(2):
-            w, c = 512 * (2 * h + k), 512 * (2 * k + u)
-            q.dma_start(T.y[64 * h:64 * (h + 1), c + 128 * b0:c + 128 * b1],
-                        T.yo[64 * u:64 * (u + 1), w + 128 * b0:w + 128 * b1]).then_inc(S[sem], 16)
-    store(Y, "sty", 0, 0, 0, 4)
-    store(Y, "sty", 0, 1, 0, 4)
-    store(Y, "sty", 1, 0, 0, 2)
-    store(Y, "sty", 1, 1, 0, 2)
-    store(Y, "sty", 1, 0, 2, 4)
-    store(A, "sta", 1, 1, 2, 4)
-    Y.wait_ge(S.sty, 16 * 10)
-    A.wait_ge(S.sta, 16 * 2)
-    g.wait_ge(S.loc, 2 * H * arrived)
+            Y.wait_ge(S["ev%d%d" % (q, b)], 1)
+        Y.dma_start(T.y[Q * q:Q * (q + 1), :], T.yo[:, 512 * q:512 * (q + 1)]).then_inc(S.sty, 16)
+    Y.wait_ge(S.sty, 16 * NQ)
+    g.wait_ge(S.loc, sum(len(eng) for call in plan for item, dst, eng in call))

import numpy as np
from concourse.bass import DstId, RemoteDMATransfer
from concourse.mybir import dt, AluOpType, ActivationFunctionType

N, E, NB = 4, 3, 4
Q = 32
NQ = 128 // Q
PIECES = [(0, 2), (2, 1), (3, 1)]
HANDED = ["c2", "s2"]
SPANS = {0: [(0, 4)], 1: [(0, 4)], 2: [(0, 4)], 3: [(0, 2), (2, 3), (3, 4)]}
ON_VECTOR = "s10 c00 c10 c20 c30 c31 c32 e23 e31 e33".split()
ON_SCALAR = "s00 s20 e00 e01 e02 e03 s30 s31 s32 e10 e11 e12 e13 e20 e21 e22 e30 e32".split()
WIDTHS = sorted(set(w for q0, w in PIECES))


def slot(w):
    return max(E * Q * w, 128)


SCRATCH = {
    "idrow": ("sbuf", [1, 16], "int32"),
    "idb": ("sbuf", [128, 16], "int32"),
    "io1": ("sbuf", [128, 16], "int32"),
    "io2": ("sbuf", [128, 8], "int32"),
    "io3": ("sbuf", [128, 8], "int32"),
    "low": ("sbuf", [128, 16], "int32"),
    "mask": ("sbuf", [128, 16], "float32"),
    "sub": ("sbuf", [128, 8], "int32"),
    "colf": ("sbuf", [128, 8], "float32"),
    "t16": ("sbuf", [128, 16], "float32"),
    "t8": ("sbuf", [128, 8], "float32"),
    "sel": ("sbuf", [128, 4], "float32"),
    "third": ("sbuf", [128, 4], "float32"),
    "rk": ("sbuf", [128, 4], "int32"),
    "xb": ("sbuf", [128, 2048], "bfloat16"),
    "xq": ("sbuf", [128, 512], "float8_e4m3fn_x4"),
    "xs": ("sbuf", [128, 512], "uint8"),
    "slotc": ("sbuf", [128, 2048], "float8_e4m3fn_x4"),
    "slots": ("sbuf", [128, 2048], "uint8"),
    "yo": ("sbuf", [128, 2048], "float32"),
    "ps": ("psum", [128, 4096], "float32"),
}
for w in WIDTHS:
    SCRATCH["tl%d" % w] = ("sbuf", [128, 4], "float32")
    SCRATCH["sl%d" % w] = ("sbuf", [128, 4], "float32")
    SCRATCH["off%d" % w] = ("sbuf", [128, 8 * NB], "uint16")
for pi, (q0, w) in enumerate(PIECES):
    SCRATCH["wb%d" % pi] = ("sbuf", [128, 4 * slot(w)], "bfloat16")
    SCRATCH["ws%d" % pi] = ("sbuf", [128, N * slot(w)], "uint8")
    SCRATCH["wc%d" % pi] = ("sbuf", [128, N * slot(w)], "float8_e4m3fn_x4")

SEMAPHORES = (["ldi", "ldx", "iota", "bc", "zero", "step", "offs", "offs2", "qx", "loc", "sty"]
              + ["%s%d" % (s, i) for s in ("ldw", "q", "c", "s") for i in range(len(PIECES))]
              + ["%s%d%d" % (s, q, i) for s in ("pc", "ps") for q in range(NQ) for i in range(len(SPANS[q]))]
              + ["%s%d%d" % (s, q, b) for s in ("mm", "ev") for q in range(NQ) for b in range(NB)])


def bits(engines):
    m = 0
    for e in engines:
        m |= 1 << e
    return m


def helpers(core, T, topo):
    free = [c for c in topo.cores_of(core) if c not in T.cores and topo.die(c) == topo.die(core)]
    return free[:len(HANDED)]


def to_far(src, item, T, topo):
    far = [c for c in T.cores if c not in topo.cores_of(src)]
    eng = topo.engines(src, far[0])
    half = len(eng) // 2
    return [(item, far[0], eng[:half]), (item, far[1], eng[half:])]


def hand_on(core, h, T, topo):
    return to_far(helpers(core, T, topo)[h], HANDED[h], T, topo)


def calls_of(core, T, topo):
    near = [c for c in T.cores if c != core and c in topo.cores_of(core)][0]
    off = [e for item, dst, eng in to_far(core, "c0", T, topo) for e in eng]
    on = [e for e in topo.engines(core, near) if e not in off]
    a, b = on[0::2], on[1::2]
    hc, hs = helpers(core, T, topo)
    return [to_far(core, "s0", T, topo) + [("s0", near, a)],
            to_far(core, "c0", T, topo) + [("c0", near, a)],
            to_far(core, "s1", T, topo) + [("s1", near, a), ("s2", hs, b[:2]), ("s2", near, b[2:])],
            to_far(core, "c1", T, topo) + [("c1", near, a), ("c2", hc, b)],
            [("c2", near, b)]]


def send(g, core, r, call, T, topo):
    ts = []
    for item, dst, eng in call:
        w = PIECES[int(item[1])][1]
        ap = T["w" + item][:, slot(w) * r:slot(w) * r + E * Q * w]
        ap = ap.bitcast(dt.uint8) if item[0] == "c" else ap
        rid, pid = topo.addr(dst, core)
        ts.append(RemoteDMATransfer(dst_ids=[DstId(rid=rid, pnc=pid)], dma_engine_mask=bits(eng),
                                    remote_sem=T.sem[item], src=ap, dst=ap))
    g.remote_dma_fused(ts, local_sem=T.sem.loc)


def helper_program(g, core, T, topo):
    for r, rank in enumerate(T.cores):
        if core in helpers(rank, T, topo):
            call = hand_on(rank, helpers(rank, T, topo).index(core), T, topo)
            got = sum(len(eng) for c in calls_of(rank, T, topo) for item, dst, eng in c if dst == core)
            g.wait_ge(T.sem[call[0][0]], got)
            send(g, core, r, call, T, topo)
            g.wait_ge(T.sem.loc, sum(len(eng) for item, dst, eng in call))


def rank_program(g, core, T, topo):
    r = T.rank_of(core)
    if r is None:
        return helper_program(g, core, T, topo)
    S = T.sem
    V, A, Y, P = g.vector, g.scalar, g.sync, g.tensor
    ADD, MUL = AluOpType.add, AluOpType.mult
    COPY = ActivationFunctionType.Copy

    A.dma_start(T.idrow[:], T.ids[:]).then_inc(S.ldi, 16)
    queues = [Y, Y, A, A, Y, A]
    n = 0
    for pi, (q0, w) in enumerate(PIECES):
        for m in range(E):
            a, c = 4 * Q * w * m, 512 * m + 4 * Q * q0
            queues[n % len(queues)].dma_start(T["wb%d" % pi][:, a:a + 4 * Q * w], T.wt[:, c:c + 4 * Q * w]
                                              ).then_inc(S["ldw%d" % pi], 16)
            n += 1
    Y.dma_start(T.xb[:], T.x[:]).then_inc(S.ldx, 16)

    g.iota(T.io1[:], [[0, 4], [1, 4]], 128, -1).then_inc(S.iota, 1)
    g.iota(T.io2[:], [[0, 8]], 0, 1).then_inc(S.iota, 1)
    g.iota(T.io3[:], [[4, 8]], 0, 0).then_inc(S.iota, 1)
    g.wait_ge(S.ldi, 16)
    g.partition_broadcast(T.idb[:], T.idrow[:], 128).then_inc(S.bc, 1)

    plan = calls_of(core, T, topo)
    seen = set()
    for call in plan:
        for item, dst, eng in call:
            if item[1] not in seen:
                g.wait_ge(S["q" + item[1]], 1)
                seen.add(item[1])
        send(g, core, r, call, T, topo)
    arrived = {}
    for other in T.cores:
        for call in calls_of(other, T, topo) + [hand_on(other, h, T, topo) for h in range(len(HANDED))]:
            for item, dst, eng in call:
                if dst == core:
                    arrived[item] = arrived.get(item, 0) + len(eng)

    narrow = [pi for pi, (q0, w) in enumerate(PIECES) if slot(w) > E * Q * w]
    for pi in narrow:
        V.memset(T["wb%d" % pi][:, 4 * E * Q * PIECES[pi][1]:], 0.0).then_inc(S.zero, 1)
    steps = [0]

    def step(*calls):
        for c in calls:
            c.then_inc(S.step, 1)
        steps[0] += len(calls)
        V.wait_ge(S.step, steps[0])
    V.wait_ge(S.iota, 3)
    step(V.tensor_scalar(T.low[:], T.io1[:], 3, None, AluOpType.bitwise_and),
         V.tensor_scalar(T.sub[:], T.io2[:], 15, 2, AluOpType.bitwise_and, AluOpType.logical_shift_right))
    step(V.tensor_scalar(T.mask[:], T.low[:], 0.0, None, AluOpType.is_equal),
         V.tensor_tensor(T.colf[:], T.sub[:], T.io3[:], ADD))
    V.wait_ge(S.zero, len(narrow))
    for pi, (q0, w) in enumerate(PIECES):
        own = slice(slot(w) * r, slot(w) * (r + 1))
        V.wait_ge(S["ldw%d" % pi], 16 * E)
        V.quantize_mx(T["wc%d" % pi][:, own], T["ws%d" % pi][:, own], T["wb%d" % pi][:]).then_inc(S["q%d" % pi], 1)
    V.wait_ge(S.bc, 1)
    step(V.tensor_tensor(T.t16[:], T.idb[:], T.mask[:], MUL))
    step(V.tensor_tensor(T.t8[:], T.t16[:, 0:16:2], T.t16[:, 1:16:2], ADD))
    step(V.tensor_tensor(T.sel[:], T.t8[:, 0:8:2], T.t8[:, 1:8:2], ADD))
    step(V.tensor_scalar(T.third[:], T.sel[:], -1.0, 1.0 / E, ADD, MUL),
         *[V.tensor_scalar(T["tl%d" % w][:], T.sel[:], float(Q * w), None, MUL) for w in WIDTHS])

    def offsets(w, sem):
        for b in range(NB):
            more = [T["sl%d" % w][:, b:b + 1], ADD, ADD] if slot(w) > E * Q * w else [None, ADD]
            V.tensor_scalar(T["off%d" % w][:, 8 * b:8 * b + 8], T.colf[:], T["tl%d" % w][:, b:b + 1], *more
                            ).then_inc(sem, 1)
    offsets(2, S.offs)
    step(V.tensor_copy(T.rk[:], T.third[:]))
    step(V.tensor_scalar(T.sl1[:], T.rk[:], float(slot(1) - E * Q), None, MUL))
    offsets(1, S.offs2)
    V.wait_ge(S.ldx, 16)
    V.quantize_mx(T.xq[:], T.xs[:], T.xb[:]).then_inc(S.qx, 1)

    def piece_of(q):
        return [pi for pi, (q0, w) in enumerate(PIECES) if q0 <= q < q0 + w][0]

    def run(eng, order):
        waited = set()

        def wait(sem, count):
            if sem not in waited:
                eng.wait_ge(S[sem], count)
                waited.add(sem)
        for kind, q, i in [(o[0], int(o[1]), int(o[2])) for o in order]:
            if kind == "e":
                o, c = 512 * (NB * (q % 2) + i), 512 * q + 128 * i
                wait("mm%d%d" % (q, i), 1)
                if eng is V:
                    call = V.tensor_copy(T.yo[:, c:c + 128], T.ps[:, o:o + 128])
                else:
                    call = A.activation(T.yo[:, c:c + 128], T.ps[:, o:o + 128], COPY)
                call.then_inc(S["ev%d%d" % (q, i)], 1)
                continue
            pi = piece_of(q)
            q0, w = PIECES[pi]
            b0, b1 = SPANS[q][i]
            lo, hi = Q * (q - q0), slot(w) * (N - 1) + E * Q * w
            offs = T["off%d" % w][:, 8 * b0:8 * b1]
            a, b = 512 * q + 128 * b0, 512 * q + 128 * b1
            item = "%s%d" % (kind, pi)
            wait("offs" if w == 2 else "offs2", NB)
            wait("q%d" % pi, 1)
            wait(item, arrived[item])
            if kind == "c":
                call = V.tensor_copy(T.slotc[:, a:b].bitcast(dt.uint32),
                                     T["w" + item][:, lo:hi].bitcast(dt.uint32).indirect(offs))
            elif eng is V:
                call = V.tensor_copy(T.slots[:, a:b], T["w" + item][:, lo:hi].indirect(offs))
            else:
                call = A.activation(T.slots[:, a:b], T["w" + item][:, lo:hi].indirect(offs), COPY)
            call.then_inc(S["p%s%d%d" % (kind, q, i)], 1)
    run(V, ON_VECTOR)
    run(A, ON_SCALAR)

    P.wait_ge(S.qx, 1)
    for q in range(NQ):
        for i, (b0, b1) in enumerate(SPANS[q]):
            P.wait_ge(S["pc%d%d" % (q, i)], 1)
            P.wait_ge(S["ps%d%d" % (q, i)], 1)
            for b in range(b0, b1):
                if q >= 2:
                    P.wait_ge(S["ev%d%d" % (q - 2, b)], 1)
                a, o = 512 * q + 128 * b, 512 * (NB * (q % 2) + b)
                P.matmul_mx(T.ps[:, o:o + 128], T.slotc[:, a:a + 128], T.slots[:, a:a + 128],
                            T.xq[:, 128 * b:128 * (b + 1)], T.xs[:, 128 * b:128 * (b + 1)], True, True
                            ).then_inc(S["mm%d%d" % (q, b)], 1)

    for q in range(NQ):
        for b in range(NB):
            Y.wait_ge(S["ev%d%d" % (q, b)], 1)
        Y.dma_start(T.y[Q * q:Q * (q + 1), :], T.yo[:, 512 * q:512 * (q + 1)]).then_inc(S.sty, 16)
    Y.wait_ge(S.sty, 16 * NQ)
    g.wait_ge(S.loc, sum(len(eng) for call in plan for item, dst, eng in call))
